import numpy as np, ml_dtypes
CORES = [35,38,43,46]
N = 4
KT, HT, TK = 2, 1, 128
def setup_inputs(rng):
    w = (rng.standard_normal((128, KT * HT * 128), dtype=np.float32) / 8).astype(ml_dtypes.bfloat16)
    return {"x": rng.standard_normal((N, 128, KT * TK), dtype=np.float32).astype(ml_dtypes.bfloat16), "w": np.broadcast_to(w, (N,) + w.shape).copy()}
def setup_inputs_big(rng):
    d = setup_inputs(rng)
    for k in ("x", "w"): d[k] = (d[k].astype(np.float32) * 1024.0).astype(d[k].dtype)
    return d
def setup_inputs_small(rng):
    d = setup_inputs(rng)
    for k in ("x", "w"): d[k] = (d[k].astype(np.float32) * (1 / 1024.0)).astype(d[k].dtype)
    return d
def setup_inputs_apart(rng):
    d = setup_inputs(rng)
    f = (10.0 ** rng.permutation(np.linspace(-1.5, 1.5, N))).astype(np.float32).reshape(N, 1, 1)
    for k in ("x",): d[k] = (d[k].astype(np.float32) * f).astype(d[k].dtype)
    return d
def tie_inputs(x):
    x = dict(x)
    x["w"] = np.broadcast_to(x["w"][0], x["w"].shape).copy()
    return x
def reference(x, w):
    X, W = x.astype(np.float64), w.astype(np.float64)
    def hidden(r):
        return np.stack([np.maximum(sum(W[r][:, 128 * (HT * t + u):128 * (HT * t + u) + 128].T @ X[r][:, TK * t:TK * t + TK] for t in range(KT)), 0.0) for u in range(HT)])
    h = [hidden(r) for r in range(N)]
    y = np.stack([sum(h[(r - 1) % N][u].T @ h[r][u] for u in range(HT)) for r in range(N)])
    return {"y": y.astype(ml_dtypes.bfloat16 if x.dtype != np.float64 else np.float64)}

@@ -1,0 +1,65 @@
+from concourse.mybir import AluOpType
+
+P = 128
+KT = 2
+ENGINES = 8
+
+SCRATCH = {
+    "xs": ("sbuf", [P, KT * P], "bfloat16"),
+    "ws": ("sbuf", [P, KT * P], "bfloat16"),
+    "zero": ("sbuf", [P, P], "float32"),
+    "hs": ("sbuf", [P, P], "bfloat16"),
+    "hp": ("sbuf", [P, P], "bfloat16"),
+    "ys": ("sbuf", [P, P], "bfloat16"),
+    "ph": ("psum", [P, 512], "float32"),
+    "py": ("psum", [P, 512], "float32"),
+}
+SEMAPHORES = ["ld", "zs", "mm1", "hrdy", "arr", "sent", "mm2", "yrdy", "st"]
+
+
+def pick_engines(allowed, n):
+    bits = [b for b in range(allowed.bit_length()) if (allowed >> b) & 1]
+    step = len(bits) // n
+    m = 0
+    for b in bits[::step][:n]:
+        m |= 1 << b
+    return m
+
+
+def rank_program(g, core, T, topo):
+    rank = T.rank_of(core)
+    if rank is None:
+        return
+    n = len(T.cores)
+    nxt = T.cores[(rank + 1) % n]
+    if not topo.may_write(core, nxt):
+        raise ValueError("core %d may not write to core %d" % (core, nxt))
+    rid, pid, _ = topo.addr(nxt)
+    mask = pick_engines(topo.mask(core, nxt), ENGINES)
+    s = T.sem
+
+    g.sync.dma_start(T.xs[:], T.x[:]).then_inc(s.ld, 16)
+    g.scalar.dma_start(T.ws[:], T.w[:]).then_inc(s.ld, 16)
+    g.vector.memset(T.zero[:], 0.0).then_inc(s.zs, 1)
+
+    g.tensor.wait_ge(s.ld, 32)
+    for t in range(KT):
+        mm = g.tensor.matmul(T.ph[:, 0:P], T.ws[:, t * P:(t + 1) * P], T.xs[:, t * P:(t + 1) * P],
+                             t == 0, t == KT - 1)
+    mm.then_inc(s.mm1, 1)
+    g.vector.wait_ge(s.zs, 1)
+    g.vector.wait_ge(s.mm1, 1)
+    g.vector.tensor_tensor(T.hs[:], T.ph[:, 0:P], T.zero[:], AluOpType.max).then_inc(s.hrdy, 1)
+
+    g.wait_ge(s.hrdy, 1)
+    g.remote_dma(T.hp[:], T.hs[:], s.arr, s.sent, pid, rid, mask)
+
+    g.tensor.wait_ge(s.hrdy, 1)
+    g.tensor.wait_ge(s.arr, ENGINES)
+    g.tensor.matmul(T.py[:, 0:P], T.hp[:], T.hs[:], True, True).then_inc(s.mm2, 1)
+    g.vector.wait_ge(s.mm2, 1)
+    g.vector.tensor_copy(T.ys[:], T.py[:, 0:P]).then_inc(s.yrdy, 1)
+    g.sync.wait_ge(s.yrdy, 1)
+    g.sync.dma_start(T.y[:], T.ys[:]).then_inc(s.st, 16)
+    g.sync.wait_ge(s.st, 16)
+    g.wait_ge(s.sent, ENGINES)

@@ -2,19 +2,23 @@ from concourse.mybir import AluOpType
 
 P = 128
 KT = 2
+C = 32
 ENGINES = 8
 
 SCRATCH = {
-    "xs": ("sbuf", [P, KT * P], "bfloat16"),
+    "xw": ("sbuf", [P, C + KT * P], "bfloat16"),
     "ws": ("sbuf", [P, KT * P], "bfloat16"),
+    "xp": ("sbuf", [P, KT * C], "bfloat16"),
     "zero": ("sbuf", [P, P], "float32"),
     "hs": ("sbuf", [P, P], "bfloat16"),
     "hp": ("sbuf", [P, P], "bfloat16"),
     "ys": ("sbuf", [P, P], "bfloat16"),
-    "ph": ("psum", [P, 512], "float32"),
+    "pb": ("psum", [P, 512], "float32"),
+    "pa": ("psum", [P, 512], "float32"),
+    "pq": ("psum", [P, 512], "float32"),
     "py": ("psum", [P, 512], "float32"),
 }
-SEMAPHORES = ["ld", "zs", "mm1", "hrdy", "arr", "sent", "mm2", "yrdy", "st"]
+SEMAPHORES = ["lx", "lw", "zs", "mb", "ma", "mq", "my", "hb", "ha", "hq", "arrx", "arrh", "sent", "yrdy", "st"]
 
 
 def pick_engines(allowed, n):
@@ -37,29 +41,48 @@ def rank_program(g, core, T, topo):
     rid, pid, _ = topo.addr(nxt)
     mask = pick_engines(topo.mask(core, nxt), ENGINES)
     s = T.sem
+    L = P - C
 
-    g.sync.dma_start(T.xs[:], T.x[:]).then_inc(s.ld, 16)
-    g.scalar.dma_start(T.ws[:], T.w[:]).then_inc(s.ld, 16)
+    def hidden(psum, cols, done):
+        for t in range(KT):
+            mm = g.tensor.matmul(psum, T.ws[:, t * P:(t + 1) * P], cols[t], t == 0, t == KT - 1)
+        mm.then_inc(done, 1)
+
+    def clamp(out, psum, width, after, done):
+        g.vector.wait_ge(after, 1)
+        g.vector.tensor_tensor(out, psum, T.zero[:, 0:width], AluOpType.max).then_inc(done, 1)
+
+    g.sync.dma_start(T.xw[:, C:C + KT * P], T.x[:]).then_inc(s.lx, 16)
+    g.scalar.dma_start(T.xw[:, 0:C], T.x[:, P:P + C]).then_inc(s.lx, 16)
+    g.scalar.dma_start(T.ws[:], T.w[:]).then_inc(s.lw, 16)
     g.vector.memset(T.zero[:], 0.0).then_inc(s.zs, 1)
-
-    g.tensor.wait_ge(s.ld, 32)
-    for t in range(KT):
-        mm = g.tensor.matmul(T.ph[:, 0:P], T.ws[:, t * P:(t + 1) * P], T.xs[:, t * P:(t + 1) * P],
-                             t == 0, t == KT - 1)
-    mm.then_inc(s.mm1, 1)
     g.vector.wait_ge(s.zs, 1)
-    g.vector.wait_ge(s.mm1, 1)
-    g.vector.tensor_tensor(T.hs[:], T.ph[:, 0:P], T.zero[:], AluOpType.max).then_inc(s.hrdy, 1)
 
-    g.wait_ge(s.hrdy, 1)
-    g.remote_dma(T.hp[:], T.hs[:], s.arr, s.sent, pid, rid, mask)
+    g.wait_ge(s.lx, 32)
+    g.remote_dma(T.xp[:], T.xw[:, 0:KT * C], s.arrx, s.sent, pid, rid, mask)
 
-    g.tensor.wait_ge(s.hrdy, 1)
-    g.tensor.wait_ge(s.arr, ENGINES)
-    g.tensor.matmul(T.py[:, 0:P], T.hp[:], T.hs[:], True, True).then_inc(s.mm2, 1)
-    g.vector.wait_ge(s.mm2, 1)
+    g.tensor.wait_ge(s.lx, 32)
+    g.tensor.wait_ge(s.lw, 16)
+    hidden(T.pb[:, 0:L], [T.xw[:, C + t * P + C:C + (t + 1) * P] for t in range(KT)], s.mb)
+    hidden(T.pa[:, 0:C], [T.xw[:, C + t * P:C + t * P + C] for t in range(KT)], s.ma)
+    clamp(T.hs[:, C:P], T.pb[:, 0:L], L, s.mb, s.hb)
+    clamp(T.hs[:, 0:C], T.pa[:, 0:C], C, s.ma, s.ha)
+
+    g.wait_ge(s.hb, 1)
+    g.remote_dma(T.hp[:, C:P], T.hs[:, C:P], s.arrh, s.sent, pid, rid, mask)
+
+    g.tensor.wait_ge(s.arrx, ENGINES)
+    hidden(T.pq[:, 0:C], [T.xp[:, C:KT * C], T.xp[:, 0:C]], s.mq)
+    clamp(T.hp[:, 0:C], T.pq[:, 0:C], C, s.mq, s.hq)
+
+    g.tensor.wait_ge(s.hb, 1)
+    g.tensor.wait_ge(s.ha, 1)
+    g.tensor.wait_ge(s.hq, 1)
+    g.tensor.wait_ge(s.arrh, ENGINES)
+    g.tensor.matmul(T.py[:, 0:P], T.hp[:], T.hs[:], True, True).then_inc(s.my, 1)
+    g.vector.wait_ge(s.my, 1)
     g.vector.tensor_copy(T.ys[:], T.py[:, 0:P]).then_inc(s.yrdy, 1)
     g.sync.wait_ge(s.yrdy, 1)
     g.sync.dma_start(T.y[:], T.ys[:]).then_inc(s.st, 16)
     g.sync.wait_ge(s.st, 16)
-    g.wait_ge(s.sent, ENGINES)
+    g.wait_ge(s.sent, 2 * ENGINES)

@@ -1,24 +1,33 @@
-from concourse.mybir import AluOpType
+from concourse.mybir import AluOpType, ActivationFunctionType
 
 P = 128
 KT = 2
-C = 32
+C = 16
+L = P - C
+LA = 56
+H = P // 2
 ENGINES = 8
 
 SCRATCH = {
-    "xw": ("sbuf", [P, C + KT * P], "bfloat16"),
+    "xe": ("sbuf", [P, KT * C], "bfloat16"),
+    "xs": ("sbuf", [P, KT * P], "bfloat16"),
     "ws": ("sbuf", [P, KT * P], "bfloat16"),
     "xp": ("sbuf", [P, KT * C], "bfloat16"),
-    "zero": ("sbuf", [P, P], "float32"),
     "hs": ("sbuf", [P, P], "bfloat16"),
-    "hp": ("sbuf", [P, P], "bfloat16"),
+    "hl": ("sbuf", [P, L], "bfloat16"),
+    "hq": ("sbuf", [P, C], "bfloat16"),
     "ys": ("sbuf", [P, P], "bfloat16"),
-    "pb": ("psum", [P, 512], "float32"),
+    "yz": ("sbuf", [P, P], "bfloat16"),
+    "pba": ("psum", [P, 512], "float32"),
+    "pbb": ("psum", [P, 512], "float32"),
     "pa": ("psum", [P, 512], "float32"),
     "pq": ("psum", [P, 512], "float32"),
-    "py": ("psum", [P, 512], "float32"),
+    "pya": ("psum", [P, 512], "float32"),
+    "pyb": ("psum", [P, 512], "float32"),
+    "pz": ("psum", [P, 512], "float32"),
 }
-SEMAPHORES = ["lx", "lw", "zs", "mb", "ma", "mq", "my", "hb", "ha", "hq", "arrx", "arrh", "sent", "yrdy", "st"]
+SEMAPHORES = ["le", "lx", "lw", "mba", "mbb", "ma", "mq", "mya", "myb", "mz", "hba", "hbb", "ha", "hq",
+              "arrx", "arrh", "sent", "ya", "yb", "yzr", "st", "stz"]
 
 
 def pick_engines(allowed, n):
@@ -41,48 +50,65 @@ def rank_program(g, core, T, topo):
     rid, pid, _ = topo.addr(nxt)
     mask = pick_engines(topo.mask(core, nxt), ENGINES)
     s = T.sem
-    L = P - C
 
     def hidden(psum, cols, done):
         for t in range(KT):
             mm = g.tensor.matmul(psum, T.ws[:, t * P:(t + 1) * P], cols[t], t == 0, t == KT - 1)
         mm.then_inc(done, 1)
 
-    def clamp(out, psum, width, after, done):
-        g.vector.wait_ge(after, 1)
-        g.vector.tensor_tensor(out, psum, T.zero[:, 0:width], AluOpType.max).then_inc(done, 1)
+    def own(lo, hi):
+        return [T.xs[:, t * P + lo:t * P + hi] for t in range(KT)]
 
-    g.sync.dma_start(T.xw[:, C:C + KT * P], T.x[:]).then_inc(s.lx, 16)
-    g.scalar.dma_start(T.xw[:, 0:C], T.x[:, P:P + C]).then_inc(s.lx, 16)
+    g.sync.dma_start(T.xe[:, 0:C], T.x[:, 0:C]).then_inc(s.le, 16)
+    g.scalar.dma_start(T.xe[:, C:KT * C], T.x[:, P:P + C]).then_inc(s.le, 16)
+    g.sync.dma_start(T.xs[:], T.x[:]).then_inc(s.lx, 16)
     g.scalar.dma_start(T.ws[:], T.w[:]).then_inc(s.lw, 16)
-    g.vector.memset(T.zero[:], 0.0).then_inc(s.zs, 1)
-    g.vector.wait_ge(s.zs, 1)
 
-    g.wait_ge(s.lx, 32)
-    g.remote_dma(T.xp[:], T.xw[:, 0:KT * C], s.arrx, s.sent, pid, rid, mask)
+    g.wait_ge(s.le, 32)
+    g.remote_dma(T.xp[:], T.xe[:], s.arrx, s.sent, pid, rid, mask)
 
-    g.tensor.wait_ge(s.lx, 32)
+    g.tensor.wait_ge(s.lx, 16)
     g.tensor.wait_ge(s.lw, 16)
-    hidden(T.pb[:, 0:L], [T.xw[:, C + t * P + C:C + (t + 1) * P] for t in range(KT)], s.mb)
-    hidden(T.pa[:, 0:C], [T.xw[:, C + t * P:C + t * P + C] for t in range(KT)], s.ma)
-    clamp(T.hs[:, C:P], T.pb[:, 0:L], L, s.mb, s.hb)
-    clamp(T.hs[:, 0:C], T.pa[:, 0:C], C, s.ma, s.ha)
+    hidden(T.pba[:, 0:LA], own(C, C + LA), s.mba)
+    hidden(T.pbb[:, 0:L - LA], own(C + LA, P), s.mbb)
+    hidden(T.pa[:, 0:C], own(0, C), s.ma)
+    g.vector.wait_ge(s.mba, 1)
+    g.vector.tensor_scalar(T.hs[:, C:C + LA], T.pba[:, 0:LA], 0.0, None, AluOpType.max).then_inc(s.hba, 1)
+    g.scalar.wait_ge(s.mbb, 1)
+    g.scalar.activation(T.hs[:, C + LA:P], T.pbb[:, 0:L - LA], ActivationFunctionType.Relu).then_inc(s.hbb, 1)
+    g.vector.wait_ge(s.ma, 1)
+    g.vector.tensor_scalar(T.hs[:, 0:C], T.pa[:, 0:C], 0.0, None, AluOpType.max).then_inc(s.ha, 1)
 
-    g.wait_ge(s.hb, 1)
-    g.remote_dma(T.hp[:, C:P], T.hs[:, C:P], s.arrh, s.sent, pid, rid, mask)
+    g.wait_ge(s.hba, 1)
+    g.wait_ge(s.hbb, 1)
+    g.remote_dma(T.hl[:], T.hs[:, C:P], s.arrh, s.sent, pid, rid, mask)
 
     g.tensor.wait_ge(s.arrx, ENGINES)
-    hidden(T.pq[:, 0:C], [T.xp[:, C:KT * C], T.xp[:, 0:C]], s.mq)
-    clamp(T.hp[:, 0:C], T.pq[:, 0:C], C, s.mq, s.hq)
+    hidden(T.pq[:, 0:C], [T.xp[:, 0:C], T.xp[:, C:KT * C]], s.mq)
+    g.vector.wait_ge(s.mq, 1)
+    g.vector.tensor_scalar(T.hq[:], T.pq[:, 0:C], 0.0, None, AluOpType.max).then_inc(s.hq, 1)
 
-    g.tensor.wait_ge(s.hb, 1)
+    g.tensor.wait_ge(s.hba, 1)
+    g.tensor.wait_ge(s.hbb, 1)
     g.tensor.wait_ge(s.ha, 1)
-    g.tensor.wait_ge(s.hq, 1)
     g.tensor.wait_ge(s.arrh, ENGINES)
-    g.tensor.matmul(T.py[:, 0:P], T.hp[:], T.hs[:], True, True).then_inc(s.my, 1)
-    g.vector.wait_ge(s.my, 1)
-    g.vector.tensor_copy(T.ys[:], T.py[:, 0:P]).then_inc(s.yrdy, 1)
-    g.sync.wait_ge(s.yrdy, 1)
-    g.sync.dma_start(T.y[:], T.ys[:]).then_inc(s.st, 16)
-    g.sync.wait_ge(s.st, 16)
+    g.tensor.matmul(T.pyb[0:L, 0:H], T.hl[:], T.hs[:, H:P], True, True).then_inc(s.myb, 1)
+    g.tensor.matmul(T.pya[0:L, 0:H], T.hl[:], T.hs[:, 0:H], True, True).then_inc(s.mya, 1)
+    g.scalar.wait_ge(s.myb, 1)
+    g.scalar.activation(T.ys[0:L, H:P], T.pyb[0:L, 0:H], ActivationFunctionType.Copy).then_inc(s.yb, 1)
+    g.vector.wait_ge(s.mya, 1)
+    g.vector.tensor_copy(T.ys[0:L, 0:H], T.pya[0:L, 0:H]).then_inc(s.ya, 1)
+    g.scalar.wait_ge(s.yb, 1)
+    g.scalar.wait_ge(s.ya, 1)
+    g.scalar.dma_start(T.y[C:P, :], T.ys[0:L, :]).then_inc(s.st, 16)
+
+    g.tensor.wait_ge(s.hq, 1)
+    g.tensor.matmul(T.pz[0:C, 0:P], T.hq[:], T.hs[:], True, True).then_inc(s.mz, 1)
+    g.vector.wait_ge(s.mz, 1)
+    g.vector.tensor_copy(T.yz[0:C, :], T.pz[0:C, 0:P]).then_inc(s.yzr, 1)
+    g.sync.wait_ge(s.yzr, 1)
+    g.sync.dma_start(T.y[0:C, :], T.yz[0:C, :]).then_inc(s.stz, 16)
+
+    g.scalar.wait_ge(s.st, 16)
+    g.sync.wait_ge(s.stz, 16)
     g.wait_ge(s.sent, 2 * ENGINES)

from concourse.mybir import AluOpType, ActivationFunctionType

P = 128
KT = 2
C = 16
L = P - C
LA = 56
H = P // 2
ENGINES = 8

SCRATCH = {
    "xe": ("sbuf", [P, KT * C], "bfloat16"),
    "xs": ("sbuf", [P, KT * P], "bfloat16"),
    "ws": ("sbuf", [P, KT * P], "bfloat16"),
    "xp": ("sbuf", [P, KT * C], "bfloat16"),
    "hs": ("sbuf", [P, P], "bfloat16"),
    "hl": ("sbuf", [P, L], "bfloat16"),
    "hq": ("sbuf", [P, C], "bfloat16"),
    "ys": ("sbuf", [P, P], "bfloat16"),
    "yz": ("sbuf", [P, P], "bfloat16"),
    "pba": ("psum", [P, 512], "float32"),
    "pbb": ("psum", [P, 512], "float32"),
    "pa": ("psum", [P, 512], "float32"),
    "pq": ("psum", [P, 512], "float32"),
    "pya": ("psum", [P, 512], "float32"),
    "pyb": ("psum", [P, 512], "float32"),
    "pz": ("psum", [P, 512], "float32"),
}
SEMAPHORES = ["le", "lx", "lw", "mba", "mbb", "ma", "mq", "mya", "myb", "mz", "hba", "hbb", "ha", "hq",
              "arrx", "arrh", "sent", "ya", "yb", "yzr", "st", "stz"]


def pick_engines(allowed, n):
    bits = [b for b in range(allowed.bit_length()) if (allowed >> b) & 1]
    step = len(bits) // n
    m = 0
    for b in bits[::step][:n]:
        m |= 1 << b
    return m


def rank_program(g, core, T, topo):
    rank = T.rank_of(core)
    if rank is None:
        return
    n = len(T.cores)
    nxt = T.cores[(rank + 1) % n]
    if not topo.may_write(core, nxt):
        raise ValueError("core %d may not write to core %d" % (core, nxt))
    rid, pid, _ = topo.addr(nxt)
    mask = pick_engines(topo.mask(core, nxt), ENGINES)
    s = T.sem

    def hidden(psum, cols, done):
        for t in range(KT):
            mm = g.tensor.matmul(psum, T.ws[:, t * P:(t + 1) * P], cols[t], t == 0, t == KT - 1)
        mm.then_inc(done, 1)

    def own(lo, hi):
        return [T.xs[:, t * P + lo:t * P + hi] for t in range(KT)]

    g.sync.dma_start(T.xe[:, 0:C], T.x[:, 0:C]).then_inc(s.le, 16)
    g.scalar.dma_start(T.xe[:, C:KT * C], T.x[:, P:P + C]).then_inc(s.le, 16)
    g.sync.dma_start(T.xs[:], T.x[:]).then_inc(s.lx, 16)
    g.scalar.dma_start(T.ws[:], T.w[:]).then_inc(s.lw, 16)

    g.wait_ge(s.le, 32)
    g.remote_dma(T.xp[:], T.xe[:], s.arrx, s.sent, pid, rid, mask)

    g.tensor.wait_ge(s.lx, 16)
    g.tensor.wait_ge(s.lw, 16)
    hidden(T.pba[:, 0:LA], own(C, C + LA), s.mba)
    hidden(T.pbb[:, 0:L - LA], own(C + LA, P), s.mbb)
    hidden(T.pa[:, 0:C], own(0, C), s.ma)
    g.vector.wait_ge(s.mba, 1)
    g.vector.tensor_scalar(T.hs[:, C:C + LA], T.pba[:, 0:LA], 0.0, None, AluOpType.max).then_inc(s.hba, 1)
    g.scalar.wait_ge(s.mbb, 1)
    g.scalar.activation(T.hs[:, C + LA:P], T.pbb[:, 0:L - LA], ActivationFunctionType.Relu).then_inc(s.hbb, 1)
    g.vector.wait_ge(s.ma, 1)
    g.vector.tensor_scalar(T.hs[:, 0:C], T.pa[:, 0:C], 0.0, None, AluOpType.max).then_inc(s.ha, 1)

    g.wait_ge(s.hba, 1)
    g.wait_ge(s.hbb, 1)
    g.remote_dma(T.hl[:], T.hs[:, C:P], s.arrh, s.sent, pid, rid, mask)

    g.tensor.wait_ge(s.arrx, ENGINES)
    hidden(T.pq[:, 0:C], [T.xp[:, 0:C], T.xp[:, C:KT * C]], s.mq)
    g.vector.wait_ge(s.mq, 1)
    g.vector.tensor_scalar(T.hq[:], T.pq[:, 0:C], 0.0, None, AluOpType.max).then_inc(s.hq, 1)

    g.tensor.wait_ge(s.hba, 1)
    g.tensor.wait_ge(s.hbb, 1)
    g.tensor.wait_ge(s.ha, 1)
    g.tensor.wait_ge(s.arrh, ENGINES)
    g.tensor.matmul(T.pyb[0:L, 0:H], T.hl[:], T.hs[:, H:P], True, True).then_inc(s.myb, 1)
    g.tensor.matmul(T.pya[0:L, 0:H], T.hl[:], T.hs[:, 0:H], True, True).then_inc(s.mya, 1)
    g.scalar.wait_ge(s.myb, 1)
    g.scalar.activation(T.ys[0:L, H:P], T.pyb[0:L, 0:H], ActivationFunctionType.Copy).then_inc(s.yb, 1)
    g.vector.wait_ge(s.mya, 1)
    g.vector.tensor_copy(T.ys[0:L, 0:H], T.pya[0:L, 0:H]).then_inc(s.ya, 1)
    g.scalar.wait_ge(s.yb, 1)
    g.scalar.wait_ge(s.ya, 1)
    g.scalar.dma_start(T.y[C:P, :], T.ys[0:L, :]).then_inc(s.st, 16)

    g.tensor.wait_ge(s.hq, 1)
    g.tensor.matmul(T.pz[0:C, 0:P], T.hq[:], T.hs[:], True, True).then_inc(s.mz, 1)
    g.vector.wait_ge(s.mz, 1)
    g.vector.tensor_copy(T.yz[0:C, :], T.pz[0:C, 0:P]).then_inc(s.yzr, 1)
    g.sync.wait_ge(s.yzr, 1)
    g.sync.dma_start(T.y[0:C, :], T.yz[0:C, :]).then_inc(s.stz, 16)

    g.scalar.wait_ge(s.st, 16)
    g.sync.wait_ge(s.stz, 16)
    g.wait_ge(s.sent, 2 * ENGINES)
